import numpy as np
import ml_dtypes


def mxq(x, axis, fmt="e4m3"):
    dtype, down = {"e4m3": (ml_dtypes.float8_e4m3fn, 7), "e5m2": (ml_dtypes.float8_e5m2, 14)}[fmt]
    v = np.moveaxis(np.asarray(x, np.float32).astype(ml_dtypes.bfloat16).astype(np.float64), axis, -1)
    blocks = v.reshape(v.shape[:-1] + (-1, 32))
    amax = np.abs(blocks).max(-1, keepdims=True)
    byte = np.maximum(np.where(amax > 0, np.frexp(amax)[1] - 1 + 127, 0) - down, 1)
    scale = np.exp2(byte - 127.0)
    codes = (blocks / scale).astype(np.float32).astype(dtype).astype(np.float64)
    return np.moveaxis((codes * scale).reshape(v.shape), -1, axis)


WIDE = False


def mx_kscale(k):
    if not WIDE:
        return np.ones(k)
    levels = np.array([10, -10, 5, -5, 0])
    if k % 512:
        return np.exp2(np.random.permutation(np.resize(levels, k // 32))).repeat(32)
    a = np.empty((k // 512, 16))
    for p in range(k // 512):
        a[p, :8] = np.random.permutation(np.resize(levels, 8))
        for g in range(8):
            far = levels[np.abs(levels - a[p, g]) >= 10]
            a[p, g + 8] = far[np.random.randint(len(far))]
    return np.exp2(a.ravel()).repeat(32)


def f64(x):
    return np.asarray(x).astype(np.float64)


def striped(idx):
    return np.tile(np.asarray(idx).reshape(-1, 16).T, (8, 1)).astype(np.uint16)


def unstriped(offs):
    return offs[:16].T.reshape(-1).astype(np.int64)


E2M1 = np.array([0.0, 0.5, 1.0, 1.5, 2.0, 3.0, 4.0, 6.0, -0.0, -0.5, -1.0, -1.5, -2.0, -3.0, -4.0, -6.0])


def pack_weight(w, fmt):
    k, n = w.shape
    w = f64(np.asarray(w, np.float32).astype(ml_dtypes.bfloat16)).reshape(k // 32, 32, n)
    amax = np.abs(w).max(1)
    if fmt == "e4m3":
        byte = np.frexp(amax)[1] - 1 + 127 - 7
    else:
        mant, ex = np.frexp(amax / 6.0)
        byte = np.where(mant > 0.5, ex, ex - 1) + 127
    byte = np.clip(np.where(amax > 0, byte, 1), 1, 254)
    scaled = (w * np.exp2(127.0 - byte)[:, None, :]).reshape(k, n).astype(np.float32)
    by_word = np.ascontiguousarray(scaled.reshape(k // 512, 128, 4, n).transpose(0, 1, 3, 2))
    if fmt == "e4m3":
        words = by_word.astype(ml_dtypes.float8_e4m3fn).view(np.uint8)
    else:
        c = by_word.astype(ml_dtypes.float4_e2m1fn).view(np.uint8) & 0xF
        words = (c[..., 0::2] | (c[..., 1::2] << 4)).reshape(k // 512, 128, 2 * n)
    return np.ascontiguousarray(words), np.ascontiguousarray(byte.astype(np.uint8).reshape(k // 512, 16, n))


def unpack_weight(words, scales, fmt):
    g, _, n = scales.shape
    words = np.ascontiguousarray(words).reshape(g, 128, n, -1)
    if fmt == "e4m3":
        vals = words.view(ml_dtypes.float8_e4m3fn).astype(np.float64)
    else:
        nib = np.empty((g, 128, n, 4), np.uint8)
        nib[..., 0::2] = words & 0xF
        nib[..., 1::2] = words >> 4
        vals = E2M1[nib]
    vals = vals * np.repeat(np.exp2(scales.astype(np.float64) - 127.0), 8, axis=1)[..., None]
    return vals.transpose(0, 1, 3, 2).reshape(g * 512, n)


K, I, L, S, T, N, M = 1024, 512, 512, 512, 512, 512, 512


def setup_inputs():
    n = np.random.standard_normal
    idx = np.random.randint(0, I, T)
    idx2 = np.random.randint(0, S, T)
    fk = mx_kscale(K)
    fn = mx_kscale(N)
    fl = mx_kscale(L)
    xap = pack_weight(n((K, I)) / fk[:, None], "e4m3")
    wap = pack_weight(n((K, N)) * 1 / np.sqrt(K) * fk[:, None] * fn, "e2m1")
    xbp = pack_weight(n((L, S)) / fl[:, None], "e2m1")
    wbp = pack_weight(n((L, N)) * 1 / np.sqrt(L) * fl[:, None] * fn, "e4m3")
    wmp = pack_weight(n((N, M)) * 1 / np.sqrt(N) / fn[:, None], "e2m1")
    return {
        "xa_words": xap[0],
        "xa_scales": xap[1],
        "wa_words": wap[0],
        "wa_scales": wap[1],
        "xb_words": xbp[0],
        "xb_scales": xbp[1],
        "wb_words": wbp[0],
        "wb_scales": wbp[1],
        "wm_words": wmp[0],
        "wm_scales": wmp[1],
        "offs": striped(idx),
        "offs2": striped(idx2),
    }


def reference(xa_words, xa_scales, wa_words, wa_scales, xb_words, xb_scales, wb_words, wb_scales, wm_words, wm_scales, offs, offs2):
    idx = unstriped(offs)
    idx2 = unstriped(offs2)
    xau = unpack_weight(xa_words, xa_scales, "e4m3")
    wau = unpack_weight(wa_words, wa_scales, "e2m1")
    xbu = unpack_weight(xb_words, xb_scales, "e2m1")
    wbu = unpack_weight(wb_words, wb_scales, "e4m3")
    wmu = unpack_weight(wm_words, wm_scales, "e2m1")
    za = wau.T @ xau
    zb = wbu.T @ xbu
    h1 = np.maximum(za[:, idx] + zb[:, idx2], 0.0)
    h1q = mxq(h1, 0, "e4m3")
    y = wmu.T @ h1q
    return y

@@ -1,0 +1,177 @@
+from contextlib import ExitStack
+
+import concourse.mybir as mybir
+
+K, L, N, M, T = 1024, 512, 512, 512, 512
+FLOPS = 2 * 512 * (K * N + L * N + N * M)
+
+F32 = mybir.dt.float32
+BF16 = mybir.dt.bfloat16
+I32 = mybir.dt.int32
+U32 = mybir.dt.uint32
+U16 = mybir.dt.uint16
+U8 = mybir.dt.uint8
+FP8X4 = mybir.dt.float8_e4m3fn_x4
+FP4X4 = mybir.dt.float4_e2m1fn_x4
+ADD = mybir.AluOpType.add
+RELU = mybir.ActivationFunctionType.Relu
+
+P = 128
+W = 512
+PACK = 4
+CHUNK = 128
+HALF = 256
+
+
+def tile_moe_combined_hidden_next_layer_kernel(
+    tc, xa_words, xa_scales, wa_words, wa_scales, xb_words, xb_scales, wb_words, wb_scales,
+    wm_words, wm_scales, offs, offs2, out,
+):
+    nc = tc.nc
+    with ExitStack() as ctx:
+        lists = ctx.enter_context(tc.tile_pool(name="lists", bufs=1))
+        keep = ctx.enter_context(tc.tile_pool(name="keep", bufs=1))
+        psum = ctx.enter_context(tc.psum_pool(name="psum", bufs=4))
+
+        def plane(name, passes, engine):
+            tile = keep.tile([P, passes * W], U8, name=name, align_bytes=64)
+            engine.memset(tile[:].bitcast(I32), 0)
+            return tile
+
+        def load_scales(queue, tile, scales, quadrants):
+            for q in quadrants:
+                queue.dma_start(
+                    tile[32 * q : 32 * q + 4, :].bitcast(I32).rearrange("r (z c) -> r z c", z=scales.shape[0]),
+                    scales[:, 4 * q : 4 * q + 4, :].rearrange("z r c -> r z c").bitcast(I32),
+                )
+
+        def load_words(queue, name, words):
+            passes, width = words.shape[0], words.shape[2]
+            tile = keep.tile([P, passes * width], U8, name=name, align_bytes=64)
+            queue.dma_start(
+                tile[:].bitcast(I32).rearrange("p (z c) -> p z c", z=passes),
+                words.rearrange("z p c -> p z c").bitcast(I32),
+            )
+            return tile
+
+        def by_residue(name, tile, dtype, run):
+            moved = keep.tile(list(tile.shape), U8, name=name, align_bytes=64)
+            nc.vector.tensor_copy(
+                moved[:].bitcast(dtype).rearrange("p (z r a b) -> p z a r b", r=PACK, a=P // run, b=run),
+                tile[:].bitcast(dtype).rearrange("p (z a b r) -> p z a r b", r=PACK, a=P // run, b=run),
+            )
+            return moved
+
+        wb_s_raw = plane("wb_s_raw", 1, nc.vector)
+        xb_s = plane("xb_s", 1, nc.vector)
+        wa_s_raw = plane("wa_s_raw", 2, nc.gpsimd)
+        xa_s = plane("xa_s", 2, nc.gpsimd)
+        wm_s = plane("wm_s", 1, nc.gpsimd)
+
+        wb_raw = load_words(nc.sync, "wb_raw", wb_words.rearrange("z p n t -> z p (n t)"))
+        xb_w = load_words(nc.scalar, "xb_w", xb_words)
+        load_scales(nc.sync, wb_s_raw, wb_scales, range(4))
+        load_scales(nc.scalar, xb_s, xb_scales, range(4))
+        wa_raw = load_words(nc.sync, "wa_raw", wa_words)
+        list_b = lists.tile([P, T // 16], U16, name="list_b")
+        nc.sync.dma_start(list_b[:], offs2)
+        load_scales(nc.sync, wa_s_raw, wa_scales, range(4))
+        xa_w = load_words(nc.sync, "xa_w", xa_words.rearrange("z p n t -> z p (n t)"))
+        load_scales(nc.sync, xa_s, xa_scales, range(4))
+        list_a = lists.tile([P, T // 16], U16, name="list_a")
+        nc.sync.dma_start(list_a[:], offs)
+        wm_w = load_words(nc.sync, "wm_w", wm_words)
+        load_scales(nc.sync, wm_s, wm_scales, range(4))
+
+        wb_w = by_residue("wb_w", wb_raw, I32, 4)
+        wb_s = by_residue("wb_s", wb_s_raw, U8, 16)
+        wa_w = by_residue("wa_w", wa_raw, U16, 8)
+        wa_s = by_residue("wa_s", wa_s_raw, U8, 16)
+
+        zb, za = [], []
+        for r in range(PACK):
+            bank = psum.tile([P, W], F32, name="z_bank")
+            nc.tensor.matmul_mx(
+                bank[:],
+                lhsT=wb_w[:, 4 * P * r : 4 * P * (r + 1)].bitcast(FP8X4),
+                lhsT_scale=wb_s[:, P * r : P * (r + 1)],
+                rhs=xb_w[:].bitcast(FP4X4),
+                rhs_scale=xb_s[:],
+                start=True,
+                stop=True,
+            )
+            zb.append(keep.tile([P, W], F32, name="zb%d" % r))
+            nc.scalar.copy(zb[r][:], bank[:])
+        for r in range(PACK):
+            bank = psum.tile([P, W], F32, name="z_bank")
+            for z in range(2):
+                first = W * z + P * r
+                nc.tensor.matmul_mx(
+                    bank[:],
+                    lhsT=wa_w[:, 2 * first : 2 * (first + P)].bitcast(FP4X4),
+                    lhsT_scale=wa_s[:, first : first + P],
+                    rhs=xa_w[:, 4 * W * z : 4 * W * (z + 1)].bitcast(FP8X4),
+                    rhs_scale=xa_s[:, W * z : W * (z + 1)],
+                    start=(z == 0),
+                    stop=(z == 1),
+                )
+            za.append(keep.tile([P, W], F32, name="za%d" % r))
+            nc.scalar.copy(za[r][:], bank[:])
+
+        picked = []
+        for r in range(PACK):
+            picked.append(keep.tile([P, T], F32, name="picked%d" % r))
+            for t0 in range(0, T, HALF):
+                nc.vector.tensor_copy(
+                    picked[r][:, t0 : t0 + HALF], zb[r][:].indirect(list_b[:, t0 // 16 : (t0 + HALF) // 16])
+                )
+
+        out_view = out.rearrange("(j p) t -> p j t", p=P)
+        chunks = T // CHUNK
+        for c in range(chunks):
+            t0 = c * CHUNK
+            last = c == chunks - 1
+            total = keep.tile([P, PACK, CHUNK], F32, name="total%d" % c)
+            for r in range(PACK):
+                nc.vector.tensor_tensor(
+                    total[:, r, :],
+                    za[r][:].indirect(list_a[:, t0 // 16 : (t0 + CHUNK) // 16]),
+                    picked[r][:, t0 : t0 + CHUNK],
+                    ADD,
+                )
+            hidden = keep.tile([P, CHUNK * PACK], BF16, name="hidden%d" % c, align_bytes=64)
+            woven = hidden[:].rearrange("p (a b r) -> p a r b", r=PACK, b=4)
+            planes = total[:].rearrange("p r (a b) -> p a r b", b=4)
+            if last:
+                nc.vector.tensor_scalar_max(woven, planes, 0.0)
+            else:
+                nc.scalar.activation(woven, planes, RELU)
+            codes = keep.tile([P, CHUNK], U32, name="codes%d" % c, align_bytes=64)
+            scale = keep.tile([P, CHUNK], U8, name="scale%d" % c, align_bytes=64)
+            nc.vector.quantize_mx(codes[:].bitcast(FP8X4), scale[:], hidden[:])
+            parts = 2 if last else 1
+            blocks = PACK // parts
+            for part in range(parts):
+                bank = psum.tile([P, blocks, CHUNK], F32, name="y_bank")
+                for jj in range(blocks):
+                    j = part * blocks + jj
+                    nc.tensor.matmul_mx(
+                        bank[:, jj, :],
+                        lhsT=wm_w[:, 2 * P * j : 2 * P * (j + 1)].bitcast(FP4X4),
+                        lhsT_scale=wm_s[:, P * j : P * (j + 1)],
+                        rhs=codes[:].bitcast(FP8X4),
+                        rhs_scale=scale[:],
+                        start=True,
+                        stop=True,
+                    )
+                result = keep.tile([P, blocks, CHUNK], F32, name="result%d_%d" % (c, part))
+                target = out_view[:, part * blocks : (part + 1) * blocks, t0 : t0 + CHUNK]
+                if last and part == 0:
+                    nc.vector.tensor_copy(result[:], bank[:])
+                    nc.sync.dma_start(target, result[:])
+                elif last:
+                    nc.scalar.copy(result[:], bank[:])
+                    nc.scalar.dma_start(target, result[:])
+                else:
+                    nc.scalar.copy(result[:], bank[:])
+                    nc.sync.dma_start(target, result[:])

@@ -18,7 +18,7 @@ RELU = mybir.ActivationFunctionType.Relu
 
 P = 128
 W = 512
-PACK = 4
+BLOCKS = 4
 CHUNK = 128
 HALF = 256
 
@@ -31,57 +31,63 @@ def tile_moe_combined_hidden_next_layer_kernel(
     with ExitStack() as ctx:
         lists = ctx.enter_context(tc.tile_pool(name="lists", bufs=1))
         keep = ctx.enter_context(tc.tile_pool(name="keep", bufs=1))
-        psum = ctx.enter_context(tc.psum_pool(name="psum", bufs=4))
+        psum = ctx.enter_context(tc.psum_pool(name="psum", bufs=1))
 
-        def plane(name, passes, engine):
-            tile = keep.tile([P, passes * W], U8, name=name, align_bytes=64)
-            engine.memset(tile[:].bitcast(I32), 0)
-            return tile
-
-        def load_scales(queue, tile, scales, quadrants):
-            for q in quadrants:
-                queue.dma_start(
-                    tile[32 * q : 32 * q + 4, :].bitcast(I32).rearrange("r (z c) -> r z c", z=scales.shape[0]),
-                    scales[:, 4 * q : 4 * q + 4, :].rearrange("z r c -> r z c").bitcast(I32),
-                )
-
-        def load_words(queue, name, words):
+        def load_words(name, words):
             passes, width = words.shape[0], words.shape[2]
             tile = keep.tile([P, passes * width], U8, name=name, align_bytes=64)
-            queue.dma_start(
+            nc.sync.dma_start(
                 tile[:].bitcast(I32).rearrange("p (z c) -> p z c", z=passes),
                 words.rearrange("z p c -> p z c").bitcast(I32),
             )
             return tile
 
+        def load_scales_spread(name, scales):
+            tile = keep.tile([P, W], U8, name=name, align_bytes=64)
+            for q in range(4):
+                rows = scales[0, 4 * q : 4 * q + 4, :].bitcast(I32)
+                nc.sync.dma_start(
+                    tile[32 * q : 32 * (q + 1), :].bitcast(I32), rows.unsqueeze(0).to_broadcast([8, 4, W // 4])
+                )
+            return tile
+
         def by_residue(name, tile, dtype, run):
             moved = keep.tile(list(tile.shape), U8, name=name, align_bytes=64)
             nc.vector.tensor_copy(
-                moved[:].bitcast(dtype).rearrange("p (z r a b) -> p z a r b", r=PACK, a=P // run, b=run),
-                tile[:].bitcast(dtype).rearrange("p (z a b r) -> p z a r b", r=PACK, a=P // run, b=run),
+                moved[:].bitcast(dtype).rearrange("p (z r a b) -> p z a r b", r=BLOCKS, a=P // run, b=run),
+                tile[:].bitcast(dtype).rearrange("p (z a b r) -> p z a r b", r=BLOCKS, a=P // run, b=run),
             )
             return moved
 
-        wb_s_raw = plane("wb_s_raw", 1, nc.vector)
-        xb_s = plane("xb_s", 1, nc.vector)
-        wa_s_raw = plane("wa_s_raw", 2, nc.gpsimd)
-        xa_s = plane("xa_s", 2, nc.gpsimd)
-        wm_s = plane("wm_s", 1, nc.gpsimd)
+        def zeroed_plane(name):
+            tile = keep.tile([P, 2 * W], U8, name=name, align_bytes=64)
+            nc.gpsimd.memset(tile[:].bitcast(I32), 0)
+            return tile
 
-        wb_raw = load_words(nc.sync, "wb_raw", wb_words.rearrange("z p n t -> z p (n t)"))
-        xb_w = load_words(nc.scalar, "xb_w", xb_words)
-        load_scales(nc.sync, wb_s_raw, wb_scales, range(4))
-        load_scales(nc.scalar, xb_s, xb_scales, range(4))
-        wa_raw = load_words(nc.sync, "wa_raw", wa_words)
+        def load_scales(tile, scales, quadrants):
+            for q in quadrants:
+                nc.sync.dma_start(
+                    tile[32 * q : 32 * q + 4, :].bitcast(I32).rearrange("r (z c) -> r z c", z=2),
+                    scales[:, 4 * q : 4 * q + 4, :].rearrange("z r c -> r z c").bitcast(I32),
+                )
+
+        wa_s_raw = zeroed_plane("wa_s_raw")
+        xa_s = zeroed_plane("xa_s")
+        wb_s_raw = load_scales_spread("wb_s_raw", wb_scales)
+        load_scales(wa_s_raw, wa_scales, (0, 1))
+        wb_raw = load_words("wb_raw", wb_words.rearrange("z p n t -> z p (n t)"))
+        wa_raw = load_words("wa_raw", wa_words)
+        xb_w = load_words("xb_w", xb_words)
+        xb_s = load_scales_spread("xb_s", xb_scales)
+        load_scales(wa_s_raw, wa_scales, (2, 3))
         list_b = lists.tile([P, T // 16], U16, name="list_b")
         nc.sync.dma_start(list_b[:], offs2)
-        load_scales(nc.sync, wa_s_raw, wa_scales, range(4))
-        xa_w = load_words(nc.sync, "xa_w", xa_words.rearrange("z p n t -> z p (n t)"))
-        load_scales(nc.sync, xa_s, xa_scales, range(4))
+        xa_w = load_words("xa_w", xa_words.rearrange("z p n t -> z p (n t)"))
+        load_scales(xa_s, xa_scales, range(4))
         list_a = lists.tile([P, T // 16], U16, name="list_a")
         nc.sync.dma_start(list_a[:], offs)
-        wm_w = load_words(nc.sync, "wm_w", wm_words)
-        load_scales(nc.sync, wm_s, wm_scales, range(4))
+        wm_w = load_words("wm_w", wm_words)
+        wm_s = load_scales_spread("wm_s", wm_scales)
 
         wb_w = by_residue("wb_w", wb_raw, I32, 4)
         wb_s = by_residue("wb_s", wb_s_raw, U8, 16)
@@ -89,23 +95,28 @@ def tile_moe_combined_hidden_next_layer_kernel(
         wa_s = by_residue("wa_s", wa_s_raw, U8, 16)
 
         zb, za = [], []
-        for r in range(PACK):
-            bank = psum.tile([P, W], F32, name="z_bank")
-            nc.tensor.matmul_mx(
-                bank[:],
-                lhsT=wb_w[:, 4 * P * r : 4 * P * (r + 1)].bitcast(FP8X4),
-                lhsT_scale=wb_s[:, P * r : P * (r + 1)],
-                rhs=xb_w[:].bitcast(FP4X4),
-                rhs_scale=xb_s[:],
-                start=True,
-                stop=True,
-            )
-            zb.append(keep.tile([P, W], F32, name="zb%d" % r))
-            nc.scalar.copy(zb[r][:], bank[:])
-        for r in range(PACK):
-            bank = psum.tile([P, W], F32, name="z_bank")
+        for j in range(BLOCKS):
+            zb.append(keep.tile([P, W], F32, name="zb%d" % j))
+            width = W // 2 if j == 0 else W
+            for s0 in range(0, W, width):
+                bank = psum.tile([P, width], F32, name="z_bank", tag="sums", bufs=4)
+                nc.tensor.matmul_mx(
+                    bank[:],
+                    lhsT=wb_w[:, 4 * P * j : 4 * P * (j + 1)].bitcast(FP8X4),
+                    lhsT_scale=wb_s[:, P * j : P * (j + 1)],
+                    rhs=xb_w[:, 2 * s0 : 2 * (s0 + width)].bitcast(FP4X4),
+                    rhs_scale=xb_s[:, s0 : s0 + width],
+                    start=True,
+                    stop=True,
+                )
+                if s0 > 0:
+                    nc.vector.tensor_copy(zb[j][:, s0 : s0 + width], bank[:])
+                else:
+                    nc.scalar.copy(zb[j][:, s0 : s0 + width], bank[:])
+        for j in range(BLOCKS):
+            bank = psum.tile([P, W], F32, name="z_bank", tag="sums", bufs=4)
             for z in range(2):
-                first = W * z + P * r
+                first = W * z + P * j
                 nc.tensor.matmul_mx(
                     bank[:],
                     lhsT=wa_w[:, 2 * first : 2 * (first + P)].bitcast(FP4X4),
@@ -115,63 +126,80 @@ def tile_moe_combined_hidden_next_layer_kernel(
                     start=(z == 0),
                     stop=(z == 1),
                 )
-            za.append(keep.tile([P, W], F32, name="za%d" % r))
-            nc.scalar.copy(za[r][:], bank[:])
-
-        picked = []
-        for r in range(PACK):
-            picked.append(keep.tile([P, T], F32, name="picked%d" % r))
-            for t0 in range(0, T, HALF):
-                nc.vector.tensor_copy(
-                    picked[r][:, t0 : t0 + HALF], zb[r][:].indirect(list_b[:, t0 // 16 : (t0 + HALF) // 16])
-                )
+            za.append(keep.tile([P, W], F32, name="za%d" % j))
+            nc.scalar.copy(za[j][:], bank[:])
 
         out_view = out.rearrange("(j p) t -> p j t", p=P)
         chunks = T // CHUNK
-        for c in range(chunks):
-            t0 = c * CHUNK
-            last = c == chunks - 1
-            total = keep.tile([P, PACK, CHUNK], F32, name="total%d" % c)
-            for r in range(PACK):
+        last = chunks - 1
+
+        picked_first = keep.tile([P, T], F32, name="picked_first")
+        picked_rest = keep.tile([P, 9 * CHUNK], F32, name="picked_rest", tag="wa_s_raw", align_bytes=64)
+        picked = [
+            [picked_first[:, :HALF]] + [picked_rest[:, CHUNK * k : CHUNK * k + HALF] for k in (0, 2, 4)],
+            [picked_first[:, HALF:]] + [picked_rest[:, CHUNK * k : CHUNK * k + HALF] for k in (7, 3, 5)],
+        ]
+
+        def look_up(h, j):
+            nc.vector.tensor_copy(picked[h][j], zb[j][:].indirect(list_b[:, h * HALF // 16 : (h + 1) * HALF // 16]))
+
+        for j in range(BLOCKS):
+            look_up(0, j)
+        look_up(1, 0)
+        look_up(1, 1)
+
+        def add_look_up(total, t0, width):
+            for j in range(BLOCKS):
                 nc.vector.tensor_tensor(
-                    total[:, r, :],
-                    za[r][:].indirect(list_a[:, t0 // 16 : (t0 + CHUNK) // 16]),
-                    picked[r][:, t0 : t0 + CHUNK],
+                    total[:, j, :],
+                    za[j][:].indirect(list_a[:, t0 // 16 : (t0 + width) // 16]),
+                    picked[t0 // HALF][j][:, t0 % HALF : t0 % HALF + width],
                     ADD,
                 )
-            hidden = keep.tile([P, CHUNK * PACK], BF16, name="hidden%d" % c, align_bytes=64)
-            woven = hidden[:].rearrange("p (a b r) -> p a r b", r=PACK, b=4)
-            planes = total[:].rearrange("p r (a b) -> p a r b", b=4)
-            if last:
+
+        def hidden_codes(c, total, hidden):
+            woven = hidden.rearrange("p (a b r) -> p a r b", r=BLOCKS, b=4)
+            planes = total.rearrange("p r (a b) -> p a r b", b=4)
+            if c == last:
                 nc.vector.tensor_scalar_max(woven, planes, 0.0)
             else:
                 nc.scalar.activation(woven, planes, RELU)
             codes = keep.tile([P, CHUNK], U32, name="codes%d" % c, align_bytes=64)
             scale = keep.tile([P, CHUNK], U8, name="scale%d" % c, align_bytes=64)
-            nc.vector.quantize_mx(codes[:].bitcast(FP8X4), scale[:], hidden[:])
-            parts = 2 if last else 1
-            blocks = PACK // parts
-            for part in range(parts):
-                bank = psum.tile([P, blocks, CHUNK], F32, name="y_bank")
-                for jj in range(blocks):
-                    j = part * blocks + jj
-                    nc.tensor.matmul_mx(
-                        bank[:, jj, :],
-                        lhsT=wm_w[:, 2 * P * j : 2 * P * (j + 1)].bitcast(FP4X4),
-                        lhsT_scale=wm_s[:, P * j : P * (j + 1)],
-                        rhs=codes[:].bitcast(FP8X4),
-                        rhs_scale=scale[:],
-                        start=True,
-                        stop=True,
-                    )
-                result = keep.tile([P, blocks, CHUNK], F32, name="result%d_%d" % (c, part))
-                target = out_view[:, part * blocks : (part + 1) * blocks, t0 : t0 + CHUNK]
-                if last and part == 0:
-                    nc.vector.tensor_copy(result[:], bank[:])
-                    nc.sync.dma_start(target, result[:])
-                elif last:
-                    nc.scalar.copy(result[:], bank[:])
-                    nc.scalar.dma_start(target, result[:])
-                else:
-                    nc.scalar.copy(result[:], bank[:])
-                    nc.sync.dma_start(target, result[:])
+            nc.vector.quantize_mx(codes[:].bitcast(FP8X4), scale[:], hidden)
+            return codes, scale
+
+        def next_layer(c, quantised, j0, j1, tag, copy, queue):
+            codes, scale = quantised
+            bank = psum.tile([P, j1 - j0, CHUNK], F32, name="y_bank", tag=tag)
+            for j in range(j0, j1):
+                nc.tensor.matmul_mx(
+                    bank[:, j - j0, :],
+                    lhsT=wm_w[:, 2 * P * j : 2 * P * (j + 1)].bitcast(FP4X4),
+                    lhsT_scale=wm_s[:, P * j : P * (j + 1)],
+                    rhs=codes[:].bitcast(FP8X4),
+                    rhs_scale=scale[:],
+                    start=True,
+                    stop=True,
+                )
+            result = keep.tile([P, j1 - j0, CHUNK], F32, name="result%d_%d" % (c, j0))
+            copy(result[:], bank[:])
+            queue.dma_start(out_view[:, j0:j1, c * CHUNK : (c + 1) * CHUNK], result[:])
+
+        sums = keep.tile([P, BLOCKS * HALF + CHUNK], F32, name="sums", align_bytes=64)
+        total_early = sums[:, : BLOCKS * HALF].rearrange("p (r t) -> p r t", r=BLOCKS)
+        add_look_up(total_early, 0, HALF)
+        for j in range(2, BLOCKS):
+            look_up(1, j)
+        own = [keep.tile([P, W], BF16, name="hidden%d" % c, align_bytes=64)[:] for c in range(3)]
+        hidden = own[:2] + [sums[:, BLOCKS * HALF - CHUNK :].bitcast(BF16)] + own[2:]
+        quantised = []
+        for c in range(chunks):
+            total = total_early[:, :, CHUNK * (c % 2) : CHUNK * (c % 2 + 1)]
+            if c >= 2:
+                add_look_up(total, c * CHUNK, CHUNK)
+            quantised.append(hidden_codes(c, total, hidden[c]))
+            if c > 0:
+                next_layer(c - 1, quantised[c - 1], 0, BLOCKS, "bank%d" % (c - 1), nc.scalar.copy, nc.sync)
+        next_layer(last, quantised[last], 0, 2, "bank3", nc.vector.tensor_copy, nc.sync)
+        next_layer(last, quantised[last], 2, 4, "bank0", nc.scalar.copy, nc.scalar)

from contextlib import ExitStack

import concourse.mybir as mybir

K, L, N, M, T = 1024, 512, 512, 512, 512
FLOPS = 2 * 512 * (K * N + L * N + N * M)

F32 = mybir.dt.float32
BF16 = mybir.dt.bfloat16
I32 = mybir.dt.int32
U32 = mybir.dt.uint32
U16 = mybir.dt.uint16
U8 = mybir.dt.uint8
FP8X4 = mybir.dt.float8_e4m3fn_x4
FP4X4 = mybir.dt.float4_e2m1fn_x4
ADD = mybir.AluOpType.add
RELU = mybir.ActivationFunctionType.Relu

P = 128
W = 512
BLOCKS = 4
CHUNK = 128
HALF = 256


def tile_moe_combined_hidden_next_layer_kernel(
    tc, xa_words, xa_scales, wa_words, wa_scales, xb_words, xb_scales, wb_words, wb_scales,
    wm_words, wm_scales, offs, offs2, out,
):
    nc = tc.nc
    with ExitStack() as ctx:
        lists = ctx.enter_context(tc.tile_pool(name="lists", bufs=1))
        keep = ctx.enter_context(tc.tile_pool(name="keep", bufs=1))
        psum = ctx.enter_context(tc.psum_pool(name="psum", bufs=1))

        def load_words(name, words):
            passes, width = words.shape[0], words.shape[2]
            tile = keep.tile([P, passes * width], U8, name=name, align_bytes=64)
            nc.sync.dma_start(
                tile[:].bitcast(I32).rearrange("p (z c) -> p z c", z=passes),
                words.rearrange("z p c -> p z c").bitcast(I32),
            )
            return tile

        def load_scales_spread(name, scales):
            tile = keep.tile([P, W], U8, name=name, align_bytes=64)
            for q in range(4):
                rows = scales[0, 4 * q : 4 * q + 4, :].bitcast(I32)
                nc.sync.dma_start(
                    tile[32 * q : 32 * (q + 1), :].bitcast(I32), rows.unsqueeze(0).to_broadcast([8, 4, W // 4])
                )
            return tile

        def by_residue(name, tile, dtype, run):
            moved = keep.tile(list(tile.shape), U8, name=name, align_bytes=64)
            nc.vector.tensor_copy(
                moved[:].bitcast(dtype).rearrange("p (z r a b) -> p z a r b", r=BLOCKS, a=P // run, b=run),
                tile[:].bitcast(dtype).rearrange("p (z a b r) -> p z a r b", r=BLOCKS, a=P // run, b=run),
            )
            return moved

        def zeroed_plane(name):
            tile = keep.tile([P, 2 * W], U8, name=name, align_bytes=64)
            nc.gpsimd.memset(tile[:].bitcast(I32), 0)
            return tile

        def load_scales(tile, scales, quadrants):
            for q in quadrants:
                nc.sync.dma_start(
                    tile[32 * q : 32 * q + 4, :].bitcast(I32).rearrange("r (z c) -> r z c", z=2),
                    scales[:, 4 * q : 4 * q + 4, :].rearrange("z r c -> r z c").bitcast(I32),
                )

        wa_s_raw = zeroed_plane("wa_s_raw")
        xa_s = zeroed_plane("xa_s")
        wb_s_raw = load_scales_spread("wb_s_raw", wb_scales)
        load_scales(wa_s_raw, wa_scales, (0, 1))
        wb_raw = load_words("wb_raw", wb_words.rearrange("z p n t -> z p (n t)"))
        wa_raw = load_words("wa_raw", wa_words)
        xb_w = load_words("xb_w", xb_words)
        xb_s = load_scales_spread("xb_s", xb_scales)
        load_scales(wa_s_raw, wa_scales, (2, 3))
        list_b = lists.tile([P, T // 16], U16, name="list_b")
        nc.sync.dma_start(list_b[:], offs2)
        xa_w = load_words("xa_w", xa_words.rearrange("z p n t -> z p (n t)"))
        load_scales(xa_s, xa_scales, range(4))
        list_a = lists.tile([P, T // 16], U16, name="list_a")
        nc.sync.dma_start(list_a[:], offs)
        wm_w = load_words("wm_w", wm_words)
        wm_s = load_scales_spread("wm_s", wm_scales)

        wb_w = by_residue("wb_w", wb_raw, I32, 4)
        wb_s = by_residue("wb_s", wb_s_raw, U8, 16)
        wa_w = by_residue("wa_w", wa_raw, U16, 8)
        wa_s = by_residue("wa_s", wa_s_raw, U8, 16)

        zb, za = [], []
        for j in range(BLOCKS):
            zb.append(keep.tile([P, W], F32, name="zb%d" % j))
            width = W // 2 if j == 0 else W
            for s0 in range(0, W, width):
                bank = psum.tile([P, width], F32, name="z_bank", tag="sums", bufs=4)
                nc.tensor.matmul_mx(
                    bank[:],
                    lhsT=wb_w[:, 4 * P * j : 4 * P * (j + 1)].bitcast(FP8X4),
                    lhsT_scale=wb_s[:, P * j : P * (j + 1)],
                    rhs=xb_w[:, 2 * s0 : 2 * (s0 + width)].bitcast(FP4X4),
                    rhs_scale=xb_s[:, s0 : s0 + width],
                    start=True,
                    stop=True,
                )
                if s0 > 0:
                    nc.vector.tensor_copy(zb[j][:, s0 : s0 + width], bank[:])
                else:
                    nc.scalar.copy(zb[j][:, s0 : s0 + width], bank[:])
        for j in range(BLOCKS):
            bank = psum.tile([P, W], F32, name="z_bank", tag="sums", bufs=4)
            for z in range(2):
                first = W * z + P * j
                nc.tensor.matmul_mx(
                    bank[:],
                    lhsT=wa_w[:, 2 * first : 2 * (first + P)].bitcast(FP4X4),
                    lhsT_scale=wa_s[:, first : first + P],
                    rhs=xa_w[:, 4 * W * z : 4 * W * (z + 1)].bitcast(FP8X4),
                    rhs_scale=xa_s[:, W * z : W * (z + 1)],
                    start=(z == 0),
                    stop=(z == 1),
                )
            za.append(keep.tile([P, W], F32, name="za%d" % j))
            nc.scalar.copy(za[j][:], bank[:])

        out_view = out.rearrange("(j p) t -> p j t", p=P)
        chunks = T // CHUNK
        last = chunks - 1

        picked_first = keep.tile([P, T], F32, name="picked_first")
        picked_rest = keep.tile([P, 9 * CHUNK], F32, name="picked_rest", tag="wa_s_raw", align_bytes=64)
        picked = [
            [picked_first[:, :HALF]] + [picked_rest[:, CHUNK * k : CHUNK * k + HALF] for k in (0, 2, 4)],
            [picked_first[:, HALF:]] + [picked_rest[:, CHUNK * k : CHUNK * k + HALF] for k in (7, 3, 5)],
        ]

        def look_up(h, j):
            nc.vector.tensor_copy(picked[h][j], zb[j][:].indirect(list_b[:, h * HALF // 16 : (h + 1) * HALF // 16]))

        for j in range(BLOCKS):
            look_up(0, j)
        look_up(1, 0)
        look_up(1, 1)

        def add_look_up(total, t0, width):
            for j in range(BLOCKS):
                nc.vector.tensor_tensor(
                    total[:, j, :],
                    za[j][:].indirect(list_a[:, t0 // 16 : (t0 + width) // 16]),
                    picked[t0 // HALF][j][:, t0 % HALF : t0 % HALF + width],
                    ADD,
                )

        def hidden_codes(c, total, hidden):
            woven = hidden.rearrange("p (a b r) -> p a r b", r=BLOCKS, b=4)
            planes = total.rearrange("p r (a b) -> p a r b", b=4)
            if c == last:
                nc.vector.tensor_scalar_max(woven, planes, 0.0)
            else:
                nc.scalar.activation(woven, planes, RELU)
            codes = keep.tile([P, CHUNK], U32, name="codes%d" % c, align_bytes=64)
            scale = keep.tile([P, CHUNK], U8, name="scale%d" % c, align_bytes=64)
            nc.vector.quantize_mx(codes[:].bitcast(FP8X4), scale[:], hidden)
            return codes, scale

        def next_layer(c, quantised, j0, j1, tag, copy, queue):
            codes, scale = quantised
            bank = psum.tile([P, j1 - j0, CHUNK], F32, name="y_bank", tag=tag)
            for j in range(j0, j1):
                nc.tensor.matmul_mx(
                    bank[:, j - j0, :],
                    lhsT=wm_w[:, 2 * P * j : 2 * P * (j + 1)].bitcast(FP4X4),
                    lhsT_scale=wm_s[:, P * j : P * (j + 1)],
                    rhs=codes[:].bitcast(FP8X4),
                    rhs_scale=scale[:],
                    start=True,
                    stop=True,
                )
            result = keep.tile([P, j1 - j0, CHUNK], F32, name="result%d_%d" % (c, j0))
            copy(result[:], bank[:])
            queue.dma_start(out_view[:, j0:j1, c * CHUNK : (c + 1) * CHUNK], result[:])

        sums = keep.tile([P, BLOCKS * HALF + CHUNK], F32, name="sums", align_bytes=64)
        total_early = sums[:, : BLOCKS * HALF].rearrange("p (r t) -> p r t", r=BLOCKS)
        add_look_up(total_early, 0, HALF)
        for j in range(2, BLOCKS):
            look_up(1, j)
        own = [keep.tile([P, W], BF16, name="hidden%d" % c, align_bytes=64)[:] for c in range(3)]
        hidden = own[:2] + [sums[:, BLOCKS * HALF - CHUNK :].bitcast(BF16)] + own[2:]
        quantised = []
        for c in range(chunks):
            total = total_early[:, :, CHUNK * (c % 2) : CHUNK * (c % 2 + 1)]
            if c >= 2:
                add_look_up(total, c * CHUNK, CHUNK)
            quantised.append(hidden_codes(c, total, hidden[c]))
            if c > 0:
                next_layer(c - 1, quantised[c - 1], 0, BLOCKS, "bank%d" % (c - 1), nc.scalar.copy, nc.sync)
        next_layer(last, quantised[last], 0, 2, "bank3", nc.vector.tensor_copy, nc.sync)
        next_layer(last, quantised[last], 2, 4, "bank0", nc.scalar.copy, nc.scalar)
